import numpy as np
import ml_dtypes


def mxq(x, axis, fmt="e4m3"):
    dtype, down = {"e4m3": (ml_dtypes.float8_e4m3fn, 7), "e5m2": (ml_dtypes.float8_e5m2, 14)}[fmt]
    v = np.moveaxis(np.asarray(x, np.float32).astype(ml_dtypes.bfloat16).astype(np.float64), axis, -1)
    blocks = v.reshape(v.shape[:-1] + (-1, 32))
    amax = np.abs(blocks).max(-1, keepdims=True)
    byte = np.maximum(np.where(amax > 0, np.frexp(amax)[1] - 1 + 127, 0) - down, 1)
    scale = np.exp2(byte - 127.0)
    codes = (blocks / scale).astype(np.float32).astype(dtype).astype(np.float64)
    return np.moveaxis((codes * scale).reshape(v.shape), -1, axis)


WIDE = False


def mx_kscale(k):
    if not WIDE:
        return np.ones(k)
    levels = np.array([10, -10, 5, -5, 0])
    if k % 512:
        return np.exp2(np.random.permutation(np.resize(levels, k // 32))).repeat(32)
    a = np.empty((k // 512, 16))
    for p in range(k // 512):
        a[p, :8] = np.random.permutation(np.resize(levels, 8))
        for g in range(8):
            far = levels[np.abs(levels - a[p, g]) >= 10]
            a[p, g + 8] = far[np.random.randint(len(far))]
    return np.exp2(a.ravel()).repeat(32)


def f64(x):
    return np.asarray(x).astype(np.float64)


def striped(idx):
    return np.tile(idx.reshape(-1, 16).T, (8, 1)).astype(np.uint16)


def unstriped(offs):
    return offs[:16].T.reshape(-1).astype(np.int64)


def gelu(v):
    return 0.5 * v * (1.0 + np.tanh(np.sqrt(2.0 / np.pi) * (v + 0.044715 * v**3)))


K, T, D, S, V, R, N = 512, 4096, 4, 4096, 1024, 4, 128


def setup_inputs():
    n = np.random.standard_normal
    s = mx_kscale(K)[:, None]
    return {
        "xT": (n((K, T)) * s).astype(np.float32),
        "w": (n((D, K, N)) / np.sqrt(D * K) / s[None]).astype(np.float32),
        "b": (0.3 * n((N, 1))).astype(np.float32),
        "offs": striped(np.concatenate([R * np.arange(V) + np.random.randint(0, R, V) for _ in range(D)])),
    }


def reference(xT, w, b, offs):
    idx = unstriped(offs)
    xq = mxq(f64(xT)[:, idx], 0, "e4m3")
    wq = mxq(f64(w), 1, "e4m3")
    y = sum(wq[d].T @ xq[:, d * V:(d + 1) * V] for d in range(D))
    y = gelu(y + f64(b))
    return y

from contextlib import ExitStack

import concourse.mybir as mybir

K, T, D, V, N = 512, 4096, 4, 1024, 128
P = 128
PACK = 4
HALF = 512
FLOPS = 2 * D * K * N * V

F32 = mybir.dt.float32
BF16 = mybir.dt.bfloat16
U32 = mybir.dt.uint32
U16 = mybir.dt.uint16
U8 = mybir.dt.uint8
FP8X4 = mybir.dt.float8_e4m3fn_x4
GELU = mybir.ActivationFunctionType.Gelu_apprx_tanh

CHUNKS = [(256, 256), (256, 256), (512, 512), (512, 512), (512, 512), (512, 448), (512, 448), (512, 448), (256, 192), (256, 128)]
RANGES = [(0, 128), (128, 256), (256, 512), (512, 1024)]


def tile_picked_deform_lin_gelu_def_e_kernel(tc, xT, w, b, offs, out):
    nc = tc.nc
    with ExitStack() as ctx:
        keep = ctx.enter_context(tc.tile_pool(name="keep", bufs=1))
        psum = ctx.enter_context(tc.psum_pool(name="psum", bufs=1))

        lists = keep.tile([P, D * V // 16], U16, name="lists")
        words = keep.tile([P, T], U32, name="words", align_bytes=64)
        scales = keep.tile([P, T], U8, name="scales", align_bytes=64)
        bias = keep.tile([P, 1], F32, name="bias")
        warm = keep.tile([P, 1], F32, name="warm")
        warm_out = keep.tile([P, 1], F32, name="warm_out")

        nc.vector.memset(warm[:], 0.0)
        nc.scalar.activation(warm_out[:], warm[:], GELU)
        for q in range(4):
            nc.gpsimd.memset(scales[:, q * 1024 : (q + 1) * 1024], 0)

        raws = []
        x_view = xT.rearrange("(p j) t -> p j t", j=PACK)
        start = 0
        for i, (width, share) in enumerate(CHUNKS):
            raw = keep.tile([P, PACK, width], F32, name="raw%d" % i)
            nc.sync.dma_start(out=raw[:], in_=x_view[:, :, start : start + width])
            raws.append((start, raw))
            start += width
            if i == 1:
                nc.sync.dma_start(lists[:], offs)
        w_raw = []
        for h in range(2):
            wr = keep.tile([P, 2, PACK, N], F32, name="w_raw%d" % h)
            nc.sync.dma_start(out=wr[:], in_=w[2 * h : 2 * h + 2].rearrange("d (p j) m -> p d j m", j=PACK))
            w_raw.append(wr)
        nc.sync.dma_start(out=bias[:], in_=b)

        picked = {}

        def interleave(copy, dst, src):
            copy(
                out=dst.rearrange("p (c i) t -> p c t i", i=4),
                in_=src.rearrange("p t (c i) -> p c t i", i=4),
            )

        def gather(lo, hi, t):
            h, c = divmod(lo, HALF)
            if c == 0:
                tag = "shared%d" % (t - 2) if h == 1 and t >= 2 else "pw%d_%d" % (h, t)
                pw = keep.tile([P, HALF], U32, name="pw%d_%d" % (h, t), tag=tag, align_bytes=64)
                ps = keep.tile([P, HALF], U8, name="ps%d_%d" % (h, t), align_bytes=64)
                picked[h, t] = (pw, ps)
            pw, ps = picked[h, t]
            dst = slice(c, c + hi - lo)
            part = lists[:, (t * V + lo) // 16 : (t * V + hi) // 16]
            nc.vector.tensor_copy(pw[:, dst], words[:, 0 : 4 * hi].indirect(part))
            nc.vector.tensor_copy(ps[:, dst], scales[:, 0 : 4 * hi].indirect(part))

        ranges = list(RANGES)
        for i, (width, share) in enumerate(CHUNKS):
            start, raw = raws[i]
            grouped = keep.tile([P, width, PACK], BF16, name="grouped%d" % i, align_bytes=64)
            interleave(nc.scalar.copy, grouped[:, 0:share, :], raw[:, :, 0:share])
            if share < width:
                interleave(nc.vector.tensor_copy, grouped[:, share:width, :], raw[:, :, share:width])
            nc.vector.quantize_mx(
                out=words[:, start : start + width].bitcast(FP8X4),
                scales=scales[:, start : start + width],
                in_=grouped[:].rearrange("p c t -> p (c t)"),
            )
            while ranges and 4 * ranges[0][1] <= start + width and ranges[0][1] < V:
                lo, hi = ranges.pop(0)
                for t in range(D):
                    gather(lo, hi, t)

        w_words = keep.tile([P, D * N], U32, name="w_words", align_bytes=64)
        w_scales = keep.tile([P, D * N], U8, name="w_scales", align_bytes=64)
        for g in range(2):
            w_grouped = keep.tile([P, 2, N, PACK], BF16, name="w_grouped%d" % g, tag="shared%d" % g, align_bytes=64)
            for t in range(2):
                interleave(nc.scalar.copy, w_grouped[:, t], w_raw[g][:, t])
            nc.vector.quantize_mx(
                out=w_words[:, g * 2 * N : (g + 1) * 2 * N].bitcast(FP8X4),
                scales=w_scales[:, g * 2 * N : (g + 1) * 2 * N],
                in_=w_grouped[:].rearrange("p d m t -> p (d m t)"),
            )
        lo, hi = ranges.pop(0)
        for t in range(D):
            gather(lo, hi, t)

        for h in range(2):
            acc = psum.tile([N, HALF], F32, name="acc%d" % h)
            for t in range(D):
                cols = slice(t * N, (t + 1) * N)
                nc.tensor.matmul_mx(
                    out=acc[:],
                    lhsT=w_words[:, cols].bitcast(FP8X4),
                    lhsT_scale=w_scales[:, cols],
                    rhs=picked[h, t][0][:].bitcast(FP8X4),
                    rhs_scale=picked[h, t][1][:],
                    start=(t == 0),
                    stop=(t == D - 1),
                )
            for q in range(2):
                result = keep.tile([N, HALF // 2], F32, name="result%d_%d" % (h, q))
                nc.scalar.activation(result[:], acc[:, q * 256 : (q + 1) * 256], GELU, bias=bias[:])
                nc.sync.dma_start(out=out[:, h * HALF + q * 256 : h * HALF + (q + 1) * 256], in_=result[:])
